import numpy as np
import ml_dtypes

BF16 = ml_dtypes.bfloat16


def bf(x):
    return np.asarray(x, np.float32).astype(BF16)


def f32(x):
    return np.asarray(x, np.float32)


def f64(x):
    return np.asarray(x).astype(np.float64)


def striped(idx):
    return np.tile(idx.reshape(-1, 16).T, (8, 1))


S, K, M, N, D, V = 2048, 128, 512, 1536, 2, 768


def setup_inputs():
    return {"table": bf(np.random.standard_normal((K, S))), "w": bf(np.random.standard_normal((K, M)) / np.sqrt(D * K)), "s": f32(0.5 + np.random.random_sample((M, 1))), "b": f32(0.5 * np.random.standard_normal((M, 1))), "offs": striped(np.random.permutation(np.tile(np.arange(S), 2))[:N])}


def reference(table, w, s, b, offs):
    idx = offs[:16].T.reshape(-1)
    x = f64(table)[:, idx]
    y = f64(w).T @ sum(x[:, t * V : (t + 1) * V] for t in range(D))
    return y * f64(s) + f64(b)

@@ -1,0 +1,49 @@
+import concourse.mybir as mybir
+
+BF16, F32, U16 = mybir.dt.bfloat16, mybir.dt.float32, mybir.dt.uint16
+MULT, ADD = mybir.AluOpType.mult, mybir.AluOpType.add
+
+P = 128
+S = 2048
+M = 512
+V = 768
+D = 2
+PIECE = 384
+PER_COLUMN = 16
+N_TILES = (M // P) * (V // PIECE)
+
+FLOPS = 2 * P * M * V + P * V * (D - 1)
+
+
+def tile_gather_matmul_kernel(tc, table, w, s, b, offs, out):
+    nc = tc.nc
+    with (
+        tc.tile_pool(name="held", bufs=1) as held,
+        tc.tile_pool(name="results", bufs=N_TILES) as results,
+        tc.psum_pool(name="banks", bufs=N_TILES) as banks,
+    ):
+        offsets = held.tile([P, D * V // PER_COLUMN], U16, name="offsets")
+        nc.sync.dma_start(offsets[:], offs)
+        nodes = held.tile([P, S], BF16, name="nodes")
+        nc.scalar.dma_start(nodes[:], table)
+        weights = held.tile([P, M], BF16, name="weights")
+        nc.sync.dma_start(weights[:], w)
+
+        gain = held.tile([P, M // P], F32, name="gain")
+        shift = held.tile([P, M // P], F32, name="shift")
+        with nc.allow_non_contiguous_dma(reason="one float32 to a partition for each block of features"):
+            nc.gpsimd.dma_start(gain[:], s.rearrange("(a p) o -> p (a o)", p=P))
+            nc.gpsimd.dma_start(shift[:], b.rearrange("(a p) o -> p (a o)", p=P))
+
+        for a in range(M // P):
+            for h in range(V // PIECE):
+                bank = banks.tile([P, PIECE], F32, name="bank")
+                for t in range(D):
+                    first = (t * V + h * PIECE) // PER_COLUMN
+                    picked = nodes[:].indirect(offsets[:, first : first + PIECE // PER_COLUMN])
+                    nc.tensor.matmul(
+                        bank[:], weights[:, a * P : (a + 1) * P], picked, start=(t == 0), stop=(t == D - 1)
+                    )
+                result = results.tile([P, PIECE], F32, name="result")
+                nc.vector.tensor_scalar(result[:], bank[:], gain[:, a : a + 1], shift[:, a : a + 1], MULT, ADD)
+                nc.sync.dma_start(out[a * P : (a + 1) * P, h * PIECE : (h + 1) * PIECE], result[:])

@@ -8,9 +8,9 @@ S = 2048
 M = 512
 V = 768
 D = 2
-PIECE = 384
+BANK = 512
+PIECES = (BANK, V - BANK)
 PER_COLUMN = 16
-N_TILES = (M // P) * (V // PIECE)
 
 FLOPS = 2 * P * M * V + P * V * (D - 1)
 
@@ -19,8 +19,8 @@ def tile_gather_matmul_kernel(tc, table, w, s, b, offs, out):
     nc = tc.nc
     with (
         tc.tile_pool(name="held", bufs=1) as held,
-        tc.tile_pool(name="results", bufs=N_TILES) as results,
-        tc.psum_pool(name="banks", bufs=N_TILES) as banks,
+        tc.tile_pool(name="results", bufs=M // P) as results,
+        tc.psum_pool(name="banks", bufs=(M // P) * len(PIECES)) as banks,
     ):
         offsets = held.tile([P, D * V // PER_COLUMN], U16, name="offsets")
         nc.sync.dma_start(offsets[:], offs)
@@ -36,14 +36,16 @@ def tile_gather_matmul_kernel(tc, table, w, s, b, offs, out):
             nc.gpsimd.dma_start(shift[:], b.rearrange("(a p) o -> p (a o)", p=P))
 
         for a in range(M // P):
-            for h in range(V // PIECE):
-                bank = banks.tile([P, PIECE], F32, name="bank")
+            v0 = 0
+            for width in PIECES:
+                bank = banks.tile([P, BANK], F32, name="bank")
                 for t in range(D):
-                    first = (t * V + h * PIECE) // PER_COLUMN
-                    picked = nodes[:].indirect(offsets[:, first : first + PIECE // PER_COLUMN])
+                    first = (t * V + v0) // PER_COLUMN
+                    picked = nodes[:].indirect(offsets[:, first : first + width // PER_COLUMN])
                     nc.tensor.matmul(
-                        bank[:], weights[:, a * P : (a + 1) * P], picked, start=(t == 0), stop=(t == D - 1)
+                        bank[:, 0:width], weights[:, a * P : (a + 1) * P], picked, start=(t == 0), stop=(t == D - 1)
                     )
-                result = results.tile([P, PIECE], F32, name="result")
-                nc.vector.tensor_scalar(result[:], bank[:], gain[:, a : a + 1], shift[:, a : a + 1], MULT, ADD)
-                nc.sync.dma_start(out[a * P : (a + 1) * P, h * PIECE : (h + 1) * PIECE], result[:])
+                result = results.tile([P, width], F32, name=f"result{width}")
+                nc.vector.tensor_scalar(result[:], bank[:, 0:width], gain[:, a : a + 1], shift[:, a : a + 1], MULT, ADD)
+                nc.sync.dma_start(out[a * P : (a + 1) * P, v0 : v0 + width], result[:])
+                v0 += width

@@ -35,9 +35,9 @@ def tile_gather_matmul_kernel(tc, table, w, s, b, offs, out):
             nc.gpsimd.dma_start(gain[:], s.rearrange("(a p) o -> p (a o)", p=P))
             nc.gpsimd.dma_start(shift[:], b.rearrange("(a p) o -> p (a o)", p=P))
 
-        for a in range(M // P):
-            v0 = 0
-            for width in PIECES:
+        v0 = 0
+        for width in PIECES:
+            for a in range(M // P):
                 bank = banks.tile([P, BANK], F32, name="bank")
                 for t in range(D):
                     first = (t * V + v0) // PER_COLUMN
@@ -48,4 +48,4 @@ def tile_gather_matmul_kernel(tc, table, w, s, b, offs, out):
                 result = results.tile([P, width], F32, name=f"result{width}")
                 nc.vector.tensor_scalar(result[:], bank[:, 0:width], gain[:, a : a + 1], shift[:, a : a + 1], MULT, ADD)
                 nc.sync.dma_start(out[a * P : (a + 1) * P, v0 : v0 + width], result[:])
-                v0 += width
+            v0 += width

@@ -26,8 +26,12 @@ def tile_gather_matmul_kernel(tc, table, w, s, b, offs, out):
         nc.sync.dma_start(offsets[:], offs)
         nodes = held.tile([P, S], BF16, name="nodes")
         nc.scalar.dma_start(nodes[:], table)
-        weights = held.tile([P, M], BF16, name="weights")
-        nc.sync.dma_start(weights[:], w)
+        weights = []
+        for a in range(M // P):
+            block = held.tile([P, P], BF16, name=f"weights{a}")
+            queue = nc.sync if a == 0 else nc.scalar
+            queue.dma_start(block[:], w[:, a * P : (a + 1) * P])
+            weights.append(block)
 
         gain = held.tile([P, M // P], F32, name="gain")
         shift = held.tile([P, M // P], F32, name="shift")
@@ -43,7 +47,7 @@ def tile_gather_matmul_kernel(tc, table, w, s, b, offs, out):
                     first = (t * V + v0) // PER_COLUMN
                     picked = nodes[:].indirect(offsets[:, first : first + width // PER_COLUMN])
                     nc.tensor.matmul(
-                        bank[:, 0:width], weights[:, a * P : (a + 1) * P], picked, start=(t == 0), stop=(t == D - 1)
+                        bank[:, 0:width], weights[a][:], picked, start=(t == 0), stop=(t == D - 1)
                     )
                 result = results.tile([P, width], F32, name=f"result{width}")
                 nc.vector.tensor_scalar(result[:], bank[:, 0:width], gain[:, a : a + 1], shift[:, a : a + 1], MULT, ADD)

@@ -10,6 +10,7 @@ V = 768
 D = 2
 BANK = 512
 PIECES = (BANK, V - BANK)
+SQUARE = 32
 PER_COLUMN = 16
 
 FLOPS = 2 * P * M * V + P * V * (D - 1)
@@ -33,11 +34,15 @@ def tile_gather_matmul_kernel(tc, table, w, s, b, offs, out):
             queue.dma_start(block[:], w[:, a * P : (a + 1) * P])
             weights.append(block)
 
-        gain = held.tile([P, M // P], F32, name="gain")
-        shift = held.tile([P, M // P], F32, name="shift")
-        with nc.allow_non_contiguous_dma(reason="one float32 to a partition for each block of features"):
-            nc.gpsimd.dma_start(gain[:], s.rearrange("(a p) o -> p (a o)", p=P))
-            nc.gpsimd.dma_start(shift[:], b.rearrange("(a p) o -> p (a o)", p=P))
+        runs = held.tile([P, P], F32, name="runs", align_bytes=64)
+        flipped = held.tile([P, P], F32, name="flipped", align_bytes=64)
+        nc.gpsimd.memset(runs[:], 0.0)
+        for j, vector in enumerate((s, b)):
+            nc.sync.dma_start(
+                runs[j:P:SQUARE, :].rearrange("q (a i) -> q a i", i=SQUARE),
+                vector.rearrange("(a q i) o -> q a (i o)", q=P // SQUARE, i=SQUARE),
+            )
+        nc.vector.transpose(flipped[:], runs[:])
 
         v0 = 0
         for width in PIECES:
@@ -50,6 +55,8 @@ def tile_gather_matmul_kernel(tc, table, w, s, b, offs, out):
                         bank[:, 0:width], weights[a][:], picked, start=(t == 0), stop=(t == D - 1)
                     )
                 result = results.tile([P, width], F32, name=f"result{width}")
-                nc.vector.tensor_scalar(result[:], bank[:, 0:width], gain[:, a : a + 1], shift[:, a : a + 1], MULT, ADD)
+                gain = flipped[:, a * SQUARE : a * SQUARE + 1]
+                shift = flipped[:, a * SQUARE + 1 : a * SQUARE + 2]
+                nc.vector.tensor_scalar(result[:], bank[:, 0:width], gain, shift, MULT, ADD)
                 nc.sync.dma_start(out[a * P : (a + 1) * P, v0 : v0 + width], result[:])
             v0 += width

@@ -27,22 +27,21 @@ def tile_gather_matmul_kernel(tc, table, w, s, b, offs, out):
         nc.sync.dma_start(offsets[:], offs)
         nodes = held.tile([P, S], BF16, name="nodes")
         nc.scalar.dma_start(nodes[:], table)
-        weights = []
-        for a in range(M // P):
-            block = held.tile([P, P], BF16, name=f"weights{a}")
-            queue = nc.sync if a == 0 else nc.scalar
-            queue.dma_start(block[:], w[:, a * P : (a + 1) * P])
-            weights.append(block)
+        weights = [held.tile([P, P], BF16, name=f"weights{a}") for a in range(M // P)]
+        nc.sync.dma_start(weights[0][:], w[:, 0:P])
 
         runs = held.tile([P, P], F32, name="runs", align_bytes=64)
         flipped = held.tile([P, P], F32, name="flipped", align_bytes=64)
         nc.gpsimd.memset(runs[:], 0.0)
         for j, vector in enumerate((s, b)):
-            nc.sync.dma_start(
+            nc.scalar.dma_start(
                 runs[j:P:SQUARE, :].rearrange("q (a i) -> q a i", i=SQUARE),
                 vector.rearrange("(a q i) o -> q a (i o)", q=P // SQUARE, i=SQUARE),
             )
         nc.vector.transpose(flipped[:], runs[:])
+
+        for a in range(1, M // P):
+            nc.scalar.dma_start(weights[a][:], w[:, a * P : (a + 1) * P])
 
         v0 = 0
         for width in PIECES:

@@ -2,6 +2,7 @@ import concourse.mybir as mybir
 
 BF16, F32, U16 = mybir.dt.bfloat16, mybir.dt.float32, mybir.dt.uint16
 MULT, ADD = mybir.AluOpType.mult, mybir.AluOpType.add
+IDENTITY = mybir.ActivationFunctionType.Identity
 
 P = 128
 S = 2048
@@ -28,20 +29,22 @@ def tile_gather_matmul_kernel(tc, table, w, s, b, offs, out):
         nodes = held.tile([P, S], BF16, name="nodes")
         nc.scalar.dma_start(nodes[:], table)
         weights = [held.tile([P, P], BF16, name=f"weights{a}") for a in range(M // P)]
+        zero = held.tile([P, 1], F32, name="zero")
+        nc.vector.memset(zero[:], 0.0)
+        for a in range(1, M // P):
+            nc.scalar.activation(weights[a][:, 0:1], zero[:], IDENTITY)
+            nc.scalar.dma_start(weights[a][:], w[:, a * P : (a + 1) * P])
         nc.sync.dma_start(weights[0][:], w[:, 0:P])
 
         runs = held.tile([P, P], F32, name="runs", align_bytes=64)
         flipped = held.tile([P, P], F32, name="flipped", align_bytes=64)
-        nc.gpsimd.memset(runs[:], 0.0)
+        nc.scalar.activation(runs[:], zero[:].to_broadcast([P, P]), IDENTITY)
         for j, vector in enumerate((s, b)):
             nc.scalar.dma_start(
                 runs[j:P:SQUARE, :].rearrange("q (a i) -> q a i", i=SQUARE),
                 vector.rearrange("(a q i) o -> q a (i o)", q=P // SQUARE, i=SQUARE),
             )
         nc.vector.transpose(flipped[:], runs[:])
-
-        for a in range(1, M // P):
-            nc.scalar.dma_start(weights[a][:], w[:, a * P : (a + 1) * P])
 
         v0 = 0
         for width in PIECES:

import concourse.mybir as mybir

BF16, F32, U16 = mybir.dt.bfloat16, mybir.dt.float32, mybir.dt.uint16
MULT, ADD = mybir.AluOpType.mult, mybir.AluOpType.add
IDENTITY = mybir.ActivationFunctionType.Identity

P = 128
S = 2048
M = 512
V = 768
D = 2
BANK = 512
PIECES = (BANK, V - BANK)
SQUARE = 32
PER_COLUMN = 16

FLOPS = 2 * P * M * V + P * V * (D - 1)


def tile_gather_matmul_kernel(tc, table, w, s, b, offs, out):
    nc = tc.nc
    with (
        tc.tile_pool(name="held", bufs=1) as held,
        tc.tile_pool(name="results", bufs=M // P) as results,
        tc.psum_pool(name="banks", bufs=(M // P) * len(PIECES)) as banks,
    ):
        offsets = held.tile([P, D * V // PER_COLUMN], U16, name="offsets")
        nc.sync.dma_start(offsets[:], offs)
        nodes = held.tile([P, S], BF16, name="nodes")
        nc.scalar.dma_start(nodes[:], table)
        weights = [held.tile([P, P], BF16, name=f"weights{a}") for a in range(M // P)]
        zero = held.tile([P, 1], F32, name="zero")
        nc.vector.memset(zero[:], 0.0)
        for a in range(1, M // P):
            nc.scalar.activation(weights[a][:, 0:1], zero[:], IDENTITY)
            nc.scalar.dma_start(weights[a][:], w[:, a * P : (a + 1) * P])
        nc.sync.dma_start(weights[0][:], w[:, 0:P])

        runs = held.tile([P, P], F32, name="runs", align_bytes=64)
        flipped = held.tile([P, P], F32, name="flipped", align_bytes=64)
        nc.scalar.activation(runs[:], zero[:].to_broadcast([P, P]), IDENTITY)
        for j, vector in enumerate((s, b)):
            nc.scalar.dma_start(
                runs[j:P:SQUARE, :].rearrange("q (a i) -> q a i", i=SQUARE),
                vector.rearrange("(a q i) o -> q a (i o)", q=P // SQUARE, i=SQUARE),
            )
        nc.vector.transpose(flipped[:], runs[:])

        v0 = 0
        for width in PIECES:
            for a in range(M // P):
                bank = banks.tile([P, BANK], F32, name="bank")
                for t in range(D):
                    first = (t * V + v0) // PER_COLUMN
                    picked = nodes[:].indirect(offsets[:, first : first + width // PER_COLUMN])
                    nc.tensor.matmul(
                        bank[:, 0:width], weights[a][:], picked, start=(t == 0), stop=(t == D - 1)
                    )
                result = results.tile([P, width], F32, name=f"result{width}")
                gain = flipped[:, a * SQUARE : a * SQUARE + 1]
                shift = flipped[:, a * SQUARE + 1 : a * SQUARE + 2]
                nc.vector.tensor_scalar(result[:], bank[:, 0:width], gain, shift, MULT, ADD)
                nc.sync.dma_start(out[a * P : (a + 1) * P, v0 : v0 + width], result[:])
            v0 += width
